import numpy as np
import ml_dtypes


def mxq(x, axis, fmt="e4m3"):
    dtype, down = {"e4m3": (ml_dtypes.float8_e4m3fn, 7), "e5m2": (ml_dtypes.float8_e5m2, 14)}[fmt]
    v = np.moveaxis(np.asarray(x, np.float32).astype(ml_dtypes.bfloat16).astype(np.float64), axis, -1)
    blocks = v.reshape(v.shape[:-1] + (-1, 32))
    amax = np.abs(blocks).max(-1, keepdims=True)
    byte = np.maximum(np.where(amax > 0, np.frexp(amax)[1] - 1 + 127, 0) - down, 1)
    scale = np.exp2(byte - 127.0)
    codes = (blocks / scale).astype(np.float32).astype(dtype).astype(np.float64)
    return np.moveaxis((codes * scale).reshape(v.shape), -1, axis)


WIDE = False


def mx_kscale(k):
    if not WIDE:
        return np.ones(k)
    levels = np.array([10, -10, 5, -5, 0])
    if k % 512:
        return np.exp2(np.random.permutation(np.resize(levels, k // 32))).repeat(32)
    a = np.empty((k // 512, 16))
    for p in range(k // 512):
        a[p, :8] = np.random.permutation(np.resize(levels, 8))
        for g in range(8):
            far = levels[np.abs(levels - a[p, g]) >= 10]
            a[p, g + 8] = far[np.random.randint(len(far))]
    return np.exp2(a.ravel()).repeat(32)


def f64(x):
    return np.asarray(x).astype(np.float64)


def striped(idx):
    return np.tile(idx.reshape(-1, 16).T, (8, 1)).astype(np.uint16)


def unstriped(offs):
    return offs[:16].T.reshape(-1).astype(np.int64)


def striped8(idx):
    return np.concatenate([x.reshape(-1, 16).T for x in idx]).astype(np.uint16)


def runs(offs, k):
    lists = np.stack([offs[16 * r : 16 * r + 16].T.reshape(-1) for r in range(8)]).astype(np.int64)
    return lists[np.arange(k) % 512 // 64]


def pack_weight(w):
    k, n = w.shape
    w = f64(np.asarray(w, np.float32).astype(ml_dtypes.bfloat16)).reshape(k // 32, 32, n)
    amax = np.abs(w).max(1)
    byte = np.clip(np.where(amax > 0, np.frexp(amax)[1] - 1 + 127 - 7, 1), 1, 254)
    scaled = (w * np.exp2(127.0 - byte)[:, None, :]).reshape(k, n).astype(np.float32)
    words = np.ascontiguousarray(scaled.reshape(k // 512, 128, 4, n).transpose(0, 1, 3, 2)).astype(ml_dtypes.float8_e4m3fn).view(np.uint8)
    return words, np.ascontiguousarray(byte.astype(np.uint8).reshape(k // 512, 16, n))


def unpack_weight(words, scales):
    g, p, n, _ = words.shape
    vals = np.ascontiguousarray(words).view(ml_dtypes.float8_e4m3fn).astype(np.float64) * np.repeat(np.exp2(scales.astype(np.float64) - 127.0), 8, axis=1)[..., None]
    return vals.transpose(0, 1, 3, 2).reshape(g * 512, n)


E2M1 = np.array([0.0, 0.5, 1.0, 1.5, 2.0, 3.0, 4.0, 6.0, -0.0, -0.5, -1.0, -1.5, -2.0, -3.0, -4.0, -6.0])


def pack_fp4(w):
    k, n = w.shape
    w = f64(np.asarray(w, np.float32).astype(ml_dtypes.bfloat16)).reshape(k // 32, 32, n)
    amax = np.abs(w).max(1)
    mant, ex = np.frexp(amax / 6.0)
    byte = np.clip(np.where(amax > 0, np.where(mant > 0.5, ex, ex - 1) + 127, 1), 1, 254)
    scaled = (w * np.exp2(127.0 - byte)[:, None, :]).reshape(k, n).astype(np.float32)
    c = np.ascontiguousarray(scaled.reshape(k // 512, 128, 4, n).transpose(0, 1, 3, 2)).astype(ml_dtypes.float4_e2m1fn).view(np.uint8) & 0xF
    words = (c[..., 0::2] | (c[..., 1::2] << 4)).reshape(k // 512, 128, 2 * n)
    return np.ascontiguousarray(words), np.ascontiguousarray(byte.astype(np.uint8).reshape(k // 512, 16, n))


def unpack_fp4(words, scales):
    g, _, n = scales.shape
    words = np.ascontiguousarray(words).reshape(g, 128, n, 2)
    nib = np.empty((g, 128, n, 4), np.uint8)
    nib[..., 0::2] = words & 0xF
    nib[..., 1::2] = words >> 4
    vals = E2M1[nib] * np.repeat(np.exp2(scales.astype(np.float64) - 127.0), 8, axis=1)[..., None]
    return vals.transpose(0, 1, 3, 2).reshape(g * 512, n)


def planes(y):
    n, m = y.shape
    v = y.astype(np.float32).astype(ml_dtypes.bfloat16).astype(np.float64).reshape(n // 32, 32, m)
    top = np.abs(v).max(1)
    byte = np.clip(np.where(top > 0, np.frexp(top)[1] - 1 + 127 - 7, 1), 1, 254)
    codes = (v * np.exp2(127.0 - byte)[:, None, :]).reshape(n, m).astype(np.float32).astype(ml_dtypes.float8_e4m3fn).view(np.uint8)
    words = codes.reshape(n // 512, 128, 4, m).transpose(0, 1, 3, 2)
    return np.ascontiguousarray(words), np.ascontiguousarray(byte.astype(np.uint8).reshape(n // 512, 16, m))


K, T, S, N, H = 512, 2048, 512, 512, 512


def setup_inputs():
    n = np.random.standard_normal
    s = mx_kscale(K)[:, None]
    u = mx_kscale(H)
    packed_xT = pack_weight(n((K, T)) * s)
    packed_w1 = pack_fp4(n((K, H)) / np.sqrt(K) / s)
    packed_w2 = pack_fp4(n((H, N)) / np.sqrt(H) / u[:, None])
    return {
        "x_words": packed_xT[0],
        "x_scales": packed_xT[1],
        "w1_words": packed_w1[0],
        "w1_scales": packed_w1[1],
        "gn": (np.random.uniform(0.5, 1.5, (H, 1)) * u[:, None]).astype(np.float32),
        "w2_words": packed_w2[0],
        "w2_scales": packed_w2[1],
        "offs": striped(np.random.permutation(T)[:S]),
        "n1": striped8(np.stack([np.random.permutation(S) for _ in range(8)])),
        "n2": striped8(np.stack([np.random.permutation(S) for _ in range(8)])),
        "n3": striped8(np.stack([np.random.permutation(S) for _ in range(8)])),
        "n4": striped8(np.stack([np.random.permutation(S) for _ in range(8)])),
    }


def reference(x_words, x_scales, w1_words, w1_scales, gn, w2_words, w2_scales, offs, n1, n2, n3, n4):
    xq = unpack_weight(x_words, x_scales)[:, unstriped(offs)]
    y = unpack_fp4(w1_words, w1_scales).T @ xq
    pa = y[np.arange(H)[:, None], runs(n1, H)]
    pb = y[np.arange(H)[:, None], runs(n2, H)]
    z = f64(gn) * (np.maximum(np.maximum(y, pa), pb) - (0.5 * (np.minimum(np.minimum(y, pa), pb))))
    h = unpack_fp4(w2_words, w2_scales).T @ mxq(z, 0, "e4m3")
    out_0 = h - (np.minimum(h[np.arange(N)[:, None], runs(n3, N)], h[np.arange(N)[:, None], runs(n4, N)]))
    return (out_0,) + planes(out_0)

@@ -1,0 +1,210 @@
+from contextlib import ExitStack
+
+import concourse.mybir as mybir
+
+K, T, S, H, N = 512, 2048, 512, 512, 512
+FLOPS = 2 * K * H * S + 2 * H * N * S
+
+F32 = mybir.dt.float32
+BF16 = mybir.dt.bfloat16
+I32 = mybir.dt.int32
+U32 = mybir.dt.uint32
+U16 = mybir.dt.uint16
+U8 = mybir.dt.uint8
+FP8X4 = mybir.dt.float8_e4m3fn_x4
+FP4X4 = mybir.dt.float4_e2m1fn_x4
+ALU = mybir.AluOpType
+COPY = mybir.ActivationFunctionType.Copy
+
+P = 128
+PACK = 4
+QUADS = 4
+CHUNK = 256
+CHUNKS = S // CHUNK
+SCALAR_COLS = 96
+
+
+def tile_picked_layrangeunder_none_po_kernel(
+    tc, x_words, x_scales, w1_words, w1_scales, gn, w2_words, w2_scales, offs, n1, n2, n3, n4, out_0, out_1, out_2
+):
+    nc = tc.nc
+    with ExitStack() as ctx:
+        held = ctx.enter_context(tc.tile_pool(name="held", bufs=1))
+        ring = ctx.enter_context(tc.tile_pool(name="ring", bufs=3))
+        psum = ctx.enter_context(tc.psum_pool(name="psum", bufs=1))
+
+        def cols(c):
+            return slice(c * CHUNK, (c + 1) * CHUNK)
+
+        def entries(lst, c):
+            return lst[:, c * CHUNK // 16 : (c + 1) * CHUNK // 16]
+
+        def load_scale_rows(engines, tile, scales):
+            for q in range(QUADS):
+                engines[q].dma_start(out=tile[32 * q : 32 * q + 4, :].bitcast(I32), in_=scales[0, 4 * q : 4 * q + 4, :].bitcast(I32))
+
+        x_scale_table = held.tile([P, T], U8, name="x_scale_table", align_bytes=64)
+        w_scale_raw = held.tile([P, H], U8, name="w_scale_raw", align_bytes=64)
+        w_word_raw = held.tile([P, 2 * H], U8, name="w_word_raw", align_bytes=64)
+        x_word_table = held.tile([P, T], I32, name="x_word_table", align_bytes=64)
+        gain = held.tile([P, PACK], F32, name="gain")
+        nc.vector.memset(x_scale_table[:].bitcast(I32), 0)
+        nc.gpsimd.memset(w_scale_raw[:].bitcast(I32), 0)
+
+        lists = []
+        for name, src in (("offs", offs), ("n1", n1), ("n2", n2), ("n3", n3), ("n4", n4)):
+            tile = held.tile([P, S // 16], U16, name="list_" + name)
+            nc.sync.dma_start(tile[:], src)
+            lists.append(tile)
+        picked, list1, list2, list3, list4 = lists
+
+        nc.scalar.dma_start(out=w_word_raw[:].bitcast(I32), in_=w1_words[0].bitcast(I32))
+        nc.sync.dma_start(out=x_word_table[:], in_=x_words[0].rearrange("p c r -> p (c r)").bitcast(I32))
+        load_scale_rows([nc.scalar] * QUADS, x_scale_table, x_scales)
+        load_scale_rows([nc.scalar] * (QUADS - 1) + [nc.gpsimd], w_scale_raw, w1_scales)
+        nc.gpsimd.dma_start(out=gain[:], in_=gn.rearrange("(p t) o -> p (t o)", t=PACK))
+
+        def deal(name):
+            words = held.tile([P, PACK, 2 * P], U8, name=name + "_words", align_bytes=64)
+            scales = held.tile([P, PACK, P], U8, name=name + "_scales", align_bytes=64)
+            nc.vector.tensor_copy(
+                out=words[:].rearrange("p t (m b) -> p t m b", b=2),
+                in_=w_word_raw[:].rearrange("p (m t b) -> p t m b", t=PACK, b=2),
+            )
+            nc.vector.tensor_copy(out=scales[:], in_=w_scale_raw[:].rearrange("p (m t) -> p t m", t=PACK))
+            return words, scales
+
+        x_scale = held.tile([P, S], U8, name="x_scale", align_bytes=64)
+        nc.vector.tensor_copy(out=x_scale[:], in_=x_scale_table[:].indirect(picked[:]))
+        w1 = deal("w1")
+        nc.sync.dma_start(out=w_word_raw[:].bitcast(I32), in_=w2_words[0].bitcast(I32))
+        load_scale_rows([nc.sync] * QUADS, w_scale_raw, w2_scales)
+
+        def product(weights, codes, scales, c):
+            banks = []
+            for t in range(PACK):
+                bank = psum.tile([P, CHUNK], F32, name="bank", tag="bank%d_%d" % (c, t))
+                nc.tensor.matmul_mx(
+                    out=bank[:],
+                    lhsT=weights[0][:, t, :].bitcast(FP4X4),
+                    lhsT_scale=weights[1][:, t, :],
+                    rhs=codes.bitcast(FP8X4),
+                    rhs_scale=scales,
+                    start=True,
+                    stop=True,
+                )
+                banks.append(bank)
+            return banks
+
+        y_banks = []
+        for c in range(CHUNKS):
+            x_code = held.tile([P, CHUNK], I32, name="x_code%d" % c, align_bytes=64)
+            nc.vector.tensor_copy(out=x_code[:].bitcast(U32), in_=x_word_table[:].bitcast(U32).indirect(entries(picked, c)))
+            y_banks.append(product(w1, x_code[:], x_scale[:, cols(c)], c))
+        w2 = deal("w2")
+
+        units = [(c, t) for c in range(CHUNKS) for t in range(PACK)]
+
+        def interleave(engine_copy, dst, src, lo, hi):
+            engine_copy(
+                out=dst[:, lo:hi, :].rearrange("p (c i) t -> p c t i", i=4),
+                in_=src[:, :, lo:hi].rearrange("p t (c i) -> p c t i", i=4),
+            )
+
+        def round_chunk(dst, src, c):
+            if c < CHUNKS - 1:
+                interleave(nc.scalar.copy, dst, src, 0, CHUNK)
+            else:
+                interleave(nc.scalar.copy, dst, src, 0, SCALAR_COLS)
+                interleave(nc.vector.tensor_copy, dst, src, SCALAR_COLS, CHUNK)
+
+        y_window = [held.tile([P, S], F32, name="y_window%d" % t) for t in range(PACK)]
+        y_own, y_gained = {}, {}
+        for c, t in units:
+            y_own[c, t] = held.tile([P, CHUNK], F32, name="y_own%d_%d" % (c, t))
+            y_gained[c, t] = held.tile([P, CHUNK], F32, name="y_gained%d_%d" % (c, t))
+        for t in range(PACK):
+            nc.scalar.activation(y_window[t][:, cols(0)], y_banks[0][t][:], COPY, scale=0.5)
+            nc.scalar.activation(y_own[0, t][:], y_banks[0][t][:], COPY, scale=0.5)
+            nc.scalar.activation(y_window[t][:, cols(1)], y_banks[1][t][:], COPY, scale=0.5)
+        for t in range(PACK):
+            nc.scalar.activation(y_gained[0, t][:], y_own[0, t][:], COPY, scale=gain[:, t : t + 1])
+        for t in range(PACK):
+            nc.scalar.activation(y_own[1, t][:], y_banks[1][t][:], COPY, scale=0.5)
+            nc.scalar.activation(y_gained[1, t][:], y_own[1, t][:], COPY, scale=gain[:, t : t + 1])
+
+        z_planes = [held.tile([P, PACK, CHUNK], BF16, name="z_planes%d" % c) for c in range(CHUNKS)]
+        h_window = [held.tile([P, S], F32, name="h_window%d" % t) for t in range(PACK)]
+        h_own = {}
+        for c, t in units:
+            h_own[c, t] = held.tile([P, CHUNK], F32, name="h_own%d_%d" % (c, t))
+
+        def second_layer(c):
+            grouped = held.tile([P, CHUNK, PACK], BF16, name="z_grouped%d" % c, align_bytes=64)
+            codes = held.tile([P, CHUNK], I32, name="z_codes%d" % c, align_bytes=64)
+            scales = held.tile([P, CHUNK], U8, name="z_scales%d" % c, align_bytes=64)
+            round_chunk(grouped, z_planes[c], c)
+            nc.vector.quantize_mx(out=codes[:].bitcast(FP8X4), scales=scales[:], in_=grouped[:].rearrange("p c t -> p (c t)"))
+            banks = product(w2, codes[:], scales[:], c)
+            for t in range(PACK):
+                nc.scalar.activation(h_window[t][:, cols(c)], banks[t][:], COPY, scale=-1.0)
+            for t in range(PACK):
+                nc.scalar.activation(h_own[c, t][:], banks[t][:], COPY)
+
+        work = {}
+
+        def scratch(kind, u):
+            work[kind, u] = ring.tile([P, CHUNK], F32, name=kind)
+            return work[kind, u][:]
+
+        for step in range(len(units) + 2):
+            fetch = step if step < len(units) else None
+            clip = step - 1 if 0 <= step - 1 < len(units) else None
+            join = step - 2 if step >= 2 else None
+            if fetch is not None:
+                c, t = units[fetch]
+                nc.vector.tensor_tensor(scratch("da", fetch), y_window[t][:].indirect(entries(list1, c)), y_own[c, t][:], ALU.subtract)
+            if clip is not None:
+                nc.vector.scalar_tensor_tensor(scratch("top", clip), work["da", clip][:], 0.0, work["db", clip][:], ALU.max, ALU.max)
+            if join is not None:
+                nc.vector.scalar_tensor_tensor(scratch("spread", join), work["top", join][:], 2.0, work["low", join][:], ALU.mult, ALU.subtract)
+            if fetch is not None:
+                c, t = units[fetch]
+                nc.vector.tensor_tensor(scratch("db", fetch), y_window[t][:].indirect(entries(list2, c)), y_own[c, t][:], ALU.subtract)
+            if clip is not None:
+                nc.vector.scalar_tensor_tensor(scratch("low", clip), work["da", clip][:], 0.0, work["db", clip][:], ALU.min, ALU.min)
+            if join is not None:
+                c, t = units[join]
+                nc.vector.scalar_tensor_tensor(
+                    z_planes[c][:, t, :], work["spread", join][:], gain[:, t : t + 1], y_gained[c, t][:], ALU.mult, ALU.add
+                )
+                if t == PACK - 1:
+                    second_layer(c)
+
+        out_rows = out_0.rearrange("(p t) s -> p t s", t=PACK)
+        out_words = out_1[0].rearrange("p c r -> p (c r)").bitcast(I32)
+        out_scales = held.tile([P, S], U8, name="out_scales", align_bytes=64)
+        result = [held.tile([P, PACK, CHUNK], F32, name="result%d" % c) for c in range(CHUNKS)]
+        for step in range(len(units) + 1):
+            fetch = step if step < len(units) else None
+            if fetch is not None:
+                c, t = units[fetch]
+                nc.vector.tensor_tensor(scratch("ha", fetch), h_window[t][:].indirect(entries(list3, c)), h_own[c, t][:], ALU.add)
+            if step >= 1:
+                c, t = units[step - 1]
+                nc.vector.tensor_tensor(result[c][:, t, :], work["ha", step - 1][:], work["hb", step - 1][:], ALU.max)
+                nc.sync.dma_start(out=out_rows[:, t, cols(c)], in_=result[c][:, t, :])
+                if t == PACK - 1:
+                    grouped = held.tile([P, CHUNK, PACK], BF16, name="out_grouped%d" % c, align_bytes=64)
+                    codes = held.tile([P, CHUNK], I32, name="out_codes%d" % c, align_bytes=64)
+                    round_chunk(grouped, result[c], c)
+                    nc.vector.quantize_mx(
+                        out=codes[:].bitcast(FP8X4), scales=out_scales[:, cols(c)], in_=grouped[:].rearrange("p c t -> p (c t)")
+                    )
+                    nc.sync.dma_start(out=out_words[:, cols(c)], in_=codes[:])
+            if fetch is not None:
+                c, t = units[fetch]
+                nc.vector.tensor_tensor(scratch("hb", fetch), h_window[t][:].indirect(entries(list4, c)), h_own[c, t][:], ALU.add)
+        for q in range(QUADS):
+            engine = nc.scalar if q % 2 else nc.sync
+            engine.dma_start(out=out_2[0, 4 * q : 4 * q + 4, :].bitcast(I32), in_=out_scales[32 * q : 32 * q + 4, :].bitcast(I32))

@@ -19,9 +19,8 @@ COPY = mybir.ActivationFunctionType.Copy
 P = 128
 PACK = 4
 QUADS = 4
-CHUNK = 256
-CHUNKS = S // CHUNK
-SCALAR_COLS = 96
+HALF = S // 2
+PIECES = [256,128,128]
 
 
 def tile_picked_layrangeunder_none_po_kernel(
@@ -33,178 +32,196 @@ def tile_picked_layrangeunder_none_po_kernel(
         ring = ctx.enter_context(tc.tile_pool(name="ring", bufs=3))
         psum = ctx.enter_context(tc.psum_pool(name="psum", bufs=1))
 
-        def cols(c):
-            return slice(c * CHUNK, (c + 1) * CHUNK)
+        def entries(lst, lo, hi):
+            return lst[:, lo // 16 : hi // 16]
 
-        def entries(lst, c):
-            return lst[:, c * CHUNK // 16 : (c + 1) * CHUNK // 16]
-
-        def load_scale_rows(engines, tile, scales):
+        def load_scale_rows(tile, lo, scales):
             for q in range(QUADS):
-                engines[q].dma_start(out=tile[32 * q : 32 * q + 4, :].bitcast(I32), in_=scales[0, 4 * q : 4 * q + 4, :].bitcast(I32))
+                nc.sync.dma_start(
+                    out=tile[32 * q : 32 * q + 4, lo : lo + scales.shape[2]].bitcast(I32), in_=scales[0, 4 * q : 4 * q + 4, :].bitcast(I32)
+                )
 
-        x_scale_table = held.tile([P, T], U8, name="x_scale_table", align_bytes=64)
-        w_scale_raw = held.tile([P, H], U8, name="w_scale_raw", align_bytes=64)
-        w_word_raw = held.tile([P, 2 * H], U8, name="w_word_raw", align_bytes=64)
-        x_word_table = held.tile([P, T], I32, name="x_word_table", align_bytes=64)
-        gain = held.tile([P, PACK], F32, name="gain")
-        nc.vector.memset(x_scale_table[:].bitcast(I32), 0)
-        nc.gpsimd.memset(w_scale_raw[:].bitcast(I32), 0)
-
-        lists = []
-        for name, src in (("offs", offs), ("n1", n1), ("n2", n2), ("n3", n3), ("n4", n4)):
+        def load_list(name, src):
             tile = held.tile([P, S // 16], U16, name="list_" + name)
             nc.sync.dma_start(tile[:], src)
-            lists.append(tile)
-        picked, list1, list2, list3, list4 = lists
+            return tile
 
-        nc.scalar.dma_start(out=w_word_raw[:].bitcast(I32), in_=w1_words[0].bitcast(I32))
-        nc.sync.dma_start(out=x_word_table[:], in_=x_words[0].rearrange("p c r -> p (c r)").bitcast(I32))
-        load_scale_rows([nc.scalar] * QUADS, x_scale_table, x_scales)
-        load_scale_rows([nc.scalar] * (QUADS - 1) + [nc.gpsimd], w_scale_raw, w1_scales)
-        nc.gpsimd.dma_start(out=gain[:], in_=gn.rearrange("(p t) o -> p (t o)", t=PACK))
+        x_scale_table = held.tile([P, T], U8, name="x_scale_table", align_bytes=64)
+        x_word_table = held.tile([P, T], I32, name="x_word_table", align_bytes=64)
+        w_scale_raw = held.tile([P, H + N], U8, name="w_scale_raw")
+        w1_word_raw = held.tile([P, 2 * H], U8, name="w1_word_raw")
+        w2_word_raw = held.tile([P, 2 * N], U8, name="w2_word_raw")
+        gain = held.tile([P, PACK], F32, name="gain")
+        nc.gpsimd.memset(x_scale_table[:].bitcast(I32), 0)
+        nc.gpsimd.memset(w_scale_raw[:].bitcast(I32), 0)
 
-        def deal(name):
+        picked = load_list("offs", offs)
+        nc.scalar.dma_start(out=w1_word_raw[:].bitcast(I32), in_=w1_words[0].bitcast(I32))
+        nc.scalar.dma_start(out=x_word_table[:], in_=x_words[0].rearrange("p c r -> p (c r)").bitcast(I32))
+        load_scale_rows(x_scale_table, 0, x_scales)
+        load_scale_rows(w_scale_raw, 0, w1_scales)
+        list1, list2 = load_list("n1", n1), load_list("n2", n2)
+        nc.sync.dma_start(out=gain[:], in_=gn.rearrange("(p t) o -> p (t o)", t=PACK))
+        nc.sync.dma_start(out=w2_word_raw[:].bitcast(I32), in_=w2_words[0].bitcast(I32))
+        load_scale_rows(w_scale_raw, H, w2_scales)
+        list3, list4 = load_list("n3", n3), load_list("n4", n4)
+
+        windows = []
+        for t in range(PACK):
+            width = S if t == PACK - 1 else 2 * S
+            windows.append(held.tile([P, width], F32, name="window%d" % t))
+            if width > S:
+                nc.gpsimd.memset(windows[t][:, S:], 0.0)
+
+        def deal(name, raw_words, raw_scales):
             words = held.tile([P, PACK, 2 * P], U8, name=name + "_words", align_bytes=64)
             scales = held.tile([P, PACK, P], U8, name=name + "_scales", align_bytes=64)
             nc.vector.tensor_copy(
                 out=words[:].rearrange("p t (m b) -> p t m b", b=2),
-                in_=w_word_raw[:].rearrange("p (m t b) -> p t m b", t=PACK, b=2),
+                in_=raw_words.rearrange("p (m t b) -> p t m b", t=PACK, b=2),
             )
-            nc.vector.tensor_copy(out=scales[:], in_=w_scale_raw[:].rearrange("p (m t) -> p t m", t=PACK))
+            nc.vector.tensor_copy(out=scales[:], in_=raw_scales.rearrange("p (m t) -> p t m", t=PACK))
             return words, scales
+
+        def product(bank, weights, t, codes, scales):
+            nc.tensor.matmul_mx(
+                out=bank,
+                lhsT=weights[0][:, t, :].bitcast(FP4X4),
+                lhsT_scale=weights[1][:, t, :],
+                rhs=codes.bitcast(FP8X4),
+                rhs_scale=scales,
+                start=True,
+                stop=True,
+            )
 
         x_scale = held.tile([P, S], U8, name="x_scale", align_bytes=64)
         nc.vector.tensor_copy(out=x_scale[:], in_=x_scale_table[:].indirect(picked[:]))
-        w1 = deal("w1")
-        nc.sync.dma_start(out=w_word_raw[:].bitcast(I32), in_=w2_words[0].bitcast(I32))
-        load_scale_rows([nc.sync] * QUADS, w_scale_raw, w2_scales)
+        w1 = deal("w1", w1_word_raw[:], w_scale_raw[:, :H])
 
-        def product(weights, codes, scales, c):
-            banks = []
+        y_banks = {}
+        for c in range(2):
+            lo, hi = c * HALF, (c + 1) * HALF
+            x_code = held.tile([P, HALF], I32, name="x_code%d" % c, align_bytes=64)
+            nc.vector.tensor_copy(out=x_code[:].bitcast(U32), in_=x_word_table[:].bitcast(U32).indirect(entries(picked, lo, hi)))
             for t in range(PACK):
-                bank = psum.tile([P, CHUNK], F32, name="bank", tag="bank%d_%d" % (c, t))
-                nc.tensor.matmul_mx(
-                    out=bank[:],
-                    lhsT=weights[0][:, t, :].bitcast(FP4X4),
-                    lhsT_scale=weights[1][:, t, :],
-                    rhs=codes.bitcast(FP8X4),
-                    rhs_scale=scales,
-                    start=True,
-                    stop=True,
-                )
-                banks.append(bank)
-            return banks
+                y_banks[c, t] = psum.tile([P, HALF], F32, name="y_bank", tag="bank%d_%d" % (c, t))
+                product(y_banks[c, t][:], w1, t, x_code[:], x_scale[:, lo:hi])
+        w2 = deal("w2", w2_word_raw[:], w_scale_raw[:, H:])
 
-        y_banks = []
-        for c in range(CHUNKS):
-            x_code = held.tile([P, CHUNK], I32, name="x_code%d" % c, align_bytes=64)
-            nc.vector.tensor_copy(out=x_code[:].bitcast(U32), in_=x_word_table[:].bitcast(U32).indirect(entries(picked, c)))
-            y_banks.append(product(w1, x_code[:], x_scale[:, cols(c)], c))
-        w2 = deal("w2")
+        starts = [sum(PIECES[:i]) for i in range(len(PIECES))]
+        chunks = [(lo, lo + width) for lo, width in zip(starts, PIECES)]
+        units = [(t, 0, S) for t in range(PACK - 1)] + [(PACK - 1, lo, hi) for lo, hi in chunks]
 
-        units = [(c, t) for c in range(CHUNKS) for t in range(PACK)]
-
-        def interleave(engine_copy, dst, src, lo, hi):
-            engine_copy(
-                out=dst[:, lo:hi, :].rearrange("p (c i) t -> p c t i", i=4),
-                in_=src[:, :, lo:hi].rearrange("p t (c i) -> p c t i", i=4),
-            )
-
-        def round_chunk(dst, src, c):
-            if c < CHUNKS - 1:
-                interleave(nc.scalar.copy, dst, src, 0, CHUNK)
-            else:
-                interleave(nc.scalar.copy, dst, src, 0, SCALAR_COLS)
-                interleave(nc.vector.tensor_copy, dst, src, SCALAR_COLS, CHUNK)
-
-        y_window = [held.tile([P, S], F32, name="y_window%d" % t) for t in range(PACK)]
-        y_own, y_gained = {}, {}
-        for c, t in units:
-            y_own[c, t] = held.tile([P, CHUNK], F32, name="y_own%d_%d" % (c, t))
-            y_gained[c, t] = held.tile([P, CHUNK], F32, name="y_gained%d_%d" % (c, t))
+        own = [held.tile([P, S], F32, name="own%d" % t) for t in range(PACK)]
+        gained = [held.tile([P, S], F32, name="gained%d" % t) for t in range(PACK)]
         for t in range(PACK):
-            nc.scalar.activation(y_window[t][:, cols(0)], y_banks[0][t][:], COPY, scale=0.5)
-            nc.scalar.activation(y_own[0, t][:], y_banks[0][t][:], COPY, scale=0.5)
-            nc.scalar.activation(y_window[t][:, cols(1)], y_banks[1][t][:], COPY, scale=0.5)
-        for t in range(PACK):
-            nc.scalar.activation(y_gained[0, t][:], y_own[0, t][:], COPY, scale=gain[:, t : t + 1])
-        for t in range(PACK):
-            nc.scalar.activation(y_own[1, t][:], y_banks[1][t][:], COPY, scale=0.5)
-            nc.scalar.activation(y_gained[1, t][:], y_own[1, t][:], COPY, scale=gain[:, t : t + 1])
+            for c in range(2):
+                lo, hi = c * HALF, (c + 1) * HALF
+                nc.scalar.activation(windows[t][:, lo:hi], y_banks[c, t][:], COPY, scale=0.5)
+                nc.scalar.activation(own[t][:, lo:hi], y_banks[c, t][:], COPY, scale=0.5)
+            if t > 0:
+                nc.scalar.activation(gained[t - 1][:], own[t - 1][:], COPY, scale=gain[:, t - 1 : t])
+        nc.scalar.activation(gained[PACK - 1][:], own[PACK - 1][:], COPY, scale=gain[:, PACK - 1 : PACK])
 
-        z_planes = [held.tile([P, PACK, CHUNK], BF16, name="z_planes%d" % c) for c in range(CHUNKS)]
-        h_window = [held.tile([P, S], F32, name="h_window%d" % t) for t in range(PACK)]
-        h_own = {}
-        for c, t in units:
-            h_own[c, t] = held.tile([P, CHUNK], F32, name="h_own%d_%d" % (c, t))
+        def grouped_tiles(name):
+            return [held.tile([P, hi - lo, PACK], BF16, name="%s%d" % (name, lo), align_bytes=64) for lo, hi in chunks]
 
-        def second_layer(c):
-            grouped = held.tile([P, CHUNK, PACK], BF16, name="z_grouped%d" % c, align_bytes=64)
-            codes = held.tile([P, CHUNK], I32, name="z_codes%d" % c, align_bytes=64)
-            scales = held.tile([P, CHUNK], U8, name="z_scales%d" % c, align_bytes=64)
-            round_chunk(grouped, z_planes[c], c)
+        def round_pair(grouped, pair, unit):
+            t, lo, hi = unit
+            for tile, (c_lo, c_hi) in zip(grouped, chunks):
+                if lo <= c_lo and c_hi <= hi:
+                    nc.scalar.copy(out=tile[:, :, t - 1 : t + 1], in_=pair[:, :, c_lo:c_hi].rearrange("p t s -> p s t"))
+
+        h_windows = windows[:-1] + [held.tile([P, S], F32, name="h_window_last")]
+        h_own = own[:-1] + [held.tile([P, S], F32, name="h_own_last")]
+        z_pairs = [held.tile([P, 2, S], F32, name="z_pair%d" % i) for i in range(2)]
+        z_grouped = grouped_tiles("z_grouped")
+        h_banks = [psum.tile([P, S], F32, name="h_bank", tag="bank0_%d" % t) for t in range(PACK)]
+
+        def fetch_h(t, lo, hi):
+            nc.scalar.activation(h_windows[t][:, lo:hi], h_banks[t][:, lo:hi], COPY, scale=-1.0)
+            nc.scalar.activation(h_own[t][:, lo:hi], h_banks[t][:, lo:hi], COPY)
+
+        def second_layer(lo, hi):
+            codes = held.tile([P, hi - lo], I32, name="z_codes%d" % lo, align_bytes=64)
+            scales = held.tile([P, hi - lo], U8, name="z_scales%d" % lo, align_bytes=64)
+            grouped = z_grouped[starts.index(lo)]
             nc.vector.quantize_mx(out=codes[:].bitcast(FP8X4), scales=scales[:], in_=grouped[:].rearrange("p c t -> p (c t)"))
-            banks = product(w2, codes[:], scales[:], c)
             for t in range(PACK):
-                nc.scalar.activation(h_window[t][:, cols(c)], banks[t][:], COPY, scale=-1.0)
-            for t in range(PACK):
-                nc.scalar.activation(h_own[c, t][:], banks[t][:], COPY)
+                product(h_banks[t][:, lo:hi], w2, t, codes[:], scales[:])
+            fetch_h(0, lo, hi)
 
         work = {}
 
         def scratch(kind, u):
-            work[kind, u] = ring.tile([P, CHUNK], F32, name=kind)
-            return work[kind, u][:]
+            tile = ring.tile([P, S], F32, name=kind)
+            work[kind, u] = tile[:, : units[u][2] - units[u][1]]
+            return work[kind, u]
 
-        for step in range(len(units) + 2):
-            fetch = step if step < len(units) else None
-            clip = step - 1 if 0 <= step - 1 < len(units) else None
-            join = step - 2 if step >= 2 else None
-            if fetch is not None:
-                c, t = units[fetch]
-                nc.vector.tensor_tensor(scratch("da", fetch), y_window[t][:].indirect(entries(list1, c)), y_own[c, t][:], ALU.subtract)
-            if clip is not None:
-                nc.vector.scalar_tensor_tensor(scratch("top", clip), work["da", clip][:], 0.0, work["db", clip][:], ALU.max, ALU.max)
-            if join is not None:
-                nc.vector.scalar_tensor_tensor(scratch("spread", join), work["top", join][:], 2.0, work["low", join][:], ALU.mult, ALU.subtract)
-            if fetch is not None:
-                c, t = units[fetch]
-                nc.vector.tensor_tensor(scratch("db", fetch), y_window[t][:].indirect(entries(list2, c)), y_own[c, t][:], ALU.subtract)
-            if clip is not None:
-                nc.vector.scalar_tensor_tensor(scratch("low", clip), work["da", clip][:], 0.0, work["db", clip][:], ALU.min, ALU.min)
-            if join is not None:
-                c, t = units[join]
-                nc.vector.scalar_tensor_tensor(
-                    z_planes[c][:, t, :], work["spread", join][:], gain[:, t : t + 1], y_gained[c, t][:], ALU.mult, ALU.add
-                )
-                if t == PACK - 1:
-                    second_layer(c)
+        def looked_up(tiles, u, lst):
+            t, lo, hi = units[u]
+            return tiles[t][:].indirect(entries(lst, lo, hi))
+
+        def at_place(tiles, u):
+            t, lo, hi = units[u]
+            return tiles[t][:, lo:hi]
+
+        def pipeline(slots):
+            for step in range(len(units) + max(lag for lag, emit in slots)):
+                for lag, emit in slots:
+                    if 0 <= step - lag < len(units):
+                        emit(step - lag)
+
+        def finish_z(u):
+            t, lo, hi = units[u]
+            nc.vector.scalar_tensor_tensor(
+                z_pairs[t // 2][:, t % 2, lo:hi], work["spread", u], gain[:, t : t + 1], at_place(gained, u), ALU.mult, ALU.add
+            )
+            if t % 2:
+                round_pair(z_grouped, z_pairs[t // 2], units[u])
+            if t == PACK - 1:
+                second_layer(lo, hi)
+
+        pipeline(
+            [
+                (0, lambda u: nc.vector.tensor_tensor(scratch("da", u), looked_up(windows, u, list1), at_place(own, u), ALU.subtract)),
+                (1, lambda u: nc.vector.scalar_tensor_tensor(scratch("top", u), work["da", u], 0.0, work["db", u], ALU.max, ALU.max)),
+                (2, lambda u: nc.vector.scalar_tensor_tensor(scratch("spread", u), work["top", u], 2.0, work["low", u], ALU.mult, ALU.subtract)),
+                (0, lambda u: nc.vector.tensor_tensor(scratch("db", u), looked_up(windows, u, list2), at_place(own, u), ALU.subtract)),
+                (1, lambda u: nc.vector.scalar_tensor_tensor(scratch("low", u), work["da", u], 0.0, work["db", u], ALU.min, ALU.min)),
+                (2, finish_z),
+            ]
+        )
+
+        for t in range(1, PACK):
+            fetch_h(t, 0, S)
 
         out_rows = out_0.rearrange("(p t) s -> p t s", t=PACK)
         out_words = out_1[0].rearrange("p c r -> p (c r)").bitcast(I32)
         out_scales = held.tile([P, S], U8, name="out_scales", align_bytes=64)
-        result = [held.tile([P, PACK, CHUNK], F32, name="result%d" % c) for c in range(CHUNKS)]
-        for step in range(len(units) + 1):
-            fetch = step if step < len(units) else None
-            if fetch is not None:
-                c, t = units[fetch]
-                nc.vector.tensor_tensor(scratch("ha", fetch), h_window[t][:].indirect(entries(list3, c)), h_own[c, t][:], ALU.add)
-            if step >= 1:
-                c, t = units[step - 1]
-                nc.vector.tensor_tensor(result[c][:, t, :], work["ha", step - 1][:], work["hb", step - 1][:], ALU.max)
-                nc.sync.dma_start(out=out_rows[:, t, cols(c)], in_=result[c][:, t, :])
-                if t == PACK - 1:
-                    grouped = held.tile([P, CHUNK, PACK], BF16, name="out_grouped%d" % c, align_bytes=64)
-                    codes = held.tile([P, CHUNK], I32, name="out_codes%d" % c, align_bytes=64)
-                    round_chunk(grouped, result[c], c)
-                    nc.vector.quantize_mx(
-                        out=codes[:].bitcast(FP8X4), scales=out_scales[:, cols(c)], in_=grouped[:].rearrange("p c t -> p (c t)")
-                    )
-                    nc.sync.dma_start(out=out_words[:, cols(c)], in_=codes[:])
-            if fetch is not None:
-                c, t = units[fetch]
-                nc.vector.tensor_tensor(scratch("hb", fetch), h_window[t][:].indirect(entries(list4, c)), h_own[c, t][:], ALU.add)
+        out_pairs = [held.tile([P, 2, S], F32, name="out_pair%d" % i) for i in range(2)]
+        out_grouped = grouped_tiles("out_grouped")
+
+        def finish_out(u):
+            t, lo, hi = units[u]
+            result = out_pairs[t // 2][:, t % 2, lo:hi]
+            nc.vector.tensor_tensor(result, work["ha", u], work["hb", u], ALU.max)
+            if t % 2:
+                round_pair(out_grouped, out_pairs[t // 2], units[u])
+            nc.sync.dma_start(out=out_rows[:, t, lo:hi], in_=result)
+            if t == PACK - 1:
+                codes = held.tile([P, hi - lo], I32, name="out_codes%d" % lo, align_bytes=64)
+                grouped = out_grouped[starts.index(lo)]
+                nc.vector.quantize_mx(out=codes[:].bitcast(FP8X4), scales=out_scales[:, lo:hi], in_=grouped[:].rearrange("p c t -> p (c t)"))
+                nc.sync.dma_start(out=out_words[:, lo:hi], in_=codes[:])
+
+        pipeline(
+            [
+                (0, lambda u: nc.vector.tensor_tensor(scratch("ha", u), looked_up(h_windows, u, list3), at_place(h_own, u), ALU.add)),
+                (1, finish_out),
+                (0, lambda u: nc.vector.tensor_tensor(scratch("hb", u), looked_up(h_windows, u, list4), at_place(h_own, u), ALU.add)),
+            ]
+        )
         for q in range(QUADS):
             engine = nc.scalar if q % 2 else nc.sync
             engine.dma_start(out=out_2[0, 4 * q : 4 * q + 4, :].bitcast(I32), in_=out_scales[32 * q : 32 * q + 4, :].bitcast(I32))

@@ -35,9 +35,9 @@ def tile_picked_layrangeunder_none_po_kernel(
         def entries(lst, lo, hi):
             return lst[:, lo // 16 : hi // 16]
 
-        def load_scale_rows(tile, lo, scales):
-            for q in range(QUADS):
-                nc.sync.dma_start(
+        def load_scale_rows(queues, tile, lo, scales):
+            for q, queue in enumerate(queues):
+                queue.dma_start(
                     out=tile[32 * q : 32 * q + 4, lo : lo + scales.shape[2]].bitcast(I32), in_=scales[0, 4 * q : 4 * q + 4, :].bitcast(I32)
                 )
 
@@ -56,14 +56,14 @@ def tile_picked_layrangeunder_none_po_kernel(
         nc.gpsimd.memset(w_scale_raw[:].bitcast(I32), 0)
 
         picked = load_list("offs", offs)
-        nc.scalar.dma_start(out=w1_word_raw[:].bitcast(I32), in_=w1_words[0].bitcast(I32))
-        nc.scalar.dma_start(out=x_word_table[:], in_=x_words[0].rearrange("p c r -> p (c r)").bitcast(I32))
-        load_scale_rows(x_scale_table, 0, x_scales)
-        load_scale_rows(w_scale_raw, 0, w1_scales)
+        nc.sync.dma_start(out=w1_word_raw[:].bitcast(I32), in_=w1_words[0].bitcast(I32))
+        load_scale_rows([nc.sync, nc.sync, nc.scalar, nc.scalar], x_scale_table, 0, x_scales)
+        nc.sync.dma_start(out=x_word_table[:], in_=x_words[0].rearrange("p c r -> p (c r)").bitcast(I32))
+        load_scale_rows([nc.scalar] * QUADS, w_scale_raw, 0, w1_scales)
         list1, list2 = load_list("n1", n1), load_list("n2", n2)
-        nc.sync.dma_start(out=gain[:], in_=gn.rearrange("(p t) o -> p (t o)", t=PACK))
         nc.sync.dma_start(out=w2_word_raw[:].bitcast(I32), in_=w2_words[0].bitcast(I32))
-        load_scale_rows(w_scale_raw, H, w2_scales)
+        nc.sync.dma_start(out=gain[:], in_=gn.rearrange("(p t) o -> p (t o)", t=PACK))
+        load_scale_rows([nc.sync] * QUADS, w_scale_raw, H, w2_scales)
         list3, list4 = load_list("n3", n3), load_list("n4", n4)
 
         windows = []
@@ -73,14 +73,14 @@ def tile_picked_layrangeunder_none_po_kernel(
             if width > S:
                 nc.gpsimd.memset(windows[t][:, S:], 0.0)
 
-        def deal(name, raw_words, raw_scales):
+        def deal(name, raw_words, raw_scales, scale_engine):
             words = held.tile([P, PACK, 2 * P], U8, name=name + "_words", align_bytes=64)
             scales = held.tile([P, PACK, P], U8, name=name + "_scales", align_bytes=64)
             nc.vector.tensor_copy(
                 out=words[:].rearrange("p t (m b) -> p t m b", b=2),
                 in_=raw_words.rearrange("p (m t b) -> p t m b", t=PACK, b=2),
             )
-            nc.vector.tensor_copy(out=scales[:], in_=raw_scales.rearrange("p (m t) -> p t m", t=PACK))
+            scale_engine.tensor_copy(out=scales[:], in_=raw_scales.rearrange("p (m t) -> p t m", t=PACK))
             return words, scales
 
         def product(bank, weights, t, codes, scales):
@@ -96,17 +96,19 @@ def tile_picked_layrangeunder_none_po_kernel(
 
         x_scale = held.tile([P, S], U8, name="x_scale", align_bytes=64)
         nc.vector.tensor_copy(out=x_scale[:], in_=x_scale_table[:].indirect(picked[:]))
-        w1 = deal("w1", w1_word_raw[:], w_scale_raw[:, :H])
+        w1 = deal("w1", w1_word_raw[:], w_scale_raw[:, :H], nc.gpsimd)
 
+        halves = [(0, HALF), (HALF, S)]
+        x_codes = []
+        for lo, hi in halves:
+            x_codes.append(held.tile([P, HALF], I32, name="x_code%d" % lo, align_bytes=64))
+            nc.vector.tensor_copy(out=x_codes[-1][:].bitcast(U32), in_=x_word_table[:].bitcast(U32).indirect(entries(picked, lo, hi)))
         y_banks = {}
-        for c in range(2):
-            lo, hi = c * HALF, (c + 1) * HALF
-            x_code = held.tile([P, HALF], I32, name="x_code%d" % c, align_bytes=64)
-            nc.vector.tensor_copy(out=x_code[:].bitcast(U32), in_=x_word_table[:].bitcast(U32).indirect(entries(picked, lo, hi)))
-            for t in range(PACK):
+        for t in range(PACK):
+            for c, (lo, hi) in enumerate(halves):
                 y_banks[c, t] = psum.tile([P, HALF], F32, name="y_bank", tag="bank%d_%d" % (c, t))
-                product(y_banks[c, t][:], w1, t, x_code[:], x_scale[:, lo:hi])
-        w2 = deal("w2", w2_word_raw[:], w_scale_raw[:, H:])
+                product(y_banks[c, t][:], w1, t, x_codes[c][:], x_scale[:, lo:hi])
+        w2 = deal("w2", w2_word_raw[:], w_scale_raw[:, H:], nc.vector)
 
         starts = [sum(PIECES[:i]) for i in range(len(PIECES))]
         chunks = [(lo, lo + width) for lo, width in zip(starts, PIECES)]
@@ -118,7 +120,10 @@ def tile_picked_layrangeunder_none_po_kernel(
             for c in range(2):
                 lo, hi = c * HALF, (c + 1) * HALF
                 nc.scalar.activation(windows[t][:, lo:hi], y_banks[c, t][:], COPY, scale=0.5)
-                nc.scalar.activation(own[t][:, lo:hi], y_banks[c, t][:], COPY, scale=0.5)
+                if (t, c) == (0, 0):
+                    nc.vector.tensor_scalar(own[t][:, lo:hi], y_banks[c, t][:], 0.5, None, ALU.mult)
+                else:
+                    nc.scalar.activation(own[t][:, lo:hi], y_banks[c, t][:], COPY, scale=0.5)
             if t > 0:
                 nc.scalar.activation(gained[t - 1][:], own[t - 1][:], COPY, scale=gain[:, t - 1 : t])
         nc.scalar.activation(gained[PACK - 1][:], own[PACK - 1][:], COPY, scale=gain[:, PACK - 1 : PACK])
@@ -130,37 +135,51 @@ def tile_picked_layrangeunder_none_po_kernel(
             t, lo, hi = unit
             for tile, (c_lo, c_hi) in zip(grouped, chunks):
                 if lo <= c_lo and c_hi <= hi:
-                    nc.scalar.copy(out=tile[:, :, t - 1 : t + 1], in_=pair[:, :, c_lo:c_hi].rearrange("p t s -> p s t"))
+                    copy = nc.vector.tensor_copy if (t, hi) == (PACK - 1, S) else nc.scalar.copy
+                    copy(out=tile[:, :, t - 1 : t + 1], in_=pair[:, :, c_lo:c_hi].rearrange("p t s -> p s t"))
 
         h_windows = windows[:-1] + [held.tile([P, S], F32, name="h_window_last")]
         h_own = own[:-1] + [held.tile([P, S], F32, name="h_own_last")]
         z_pairs = [held.tile([P, 2, S], F32, name="z_pair%d" % i) for i in range(2)]
         z_grouped = grouped_tiles("z_grouped")
-        h_banks = [psum.tile([P, S], F32, name="h_bank", tag="bank0_%d" % t) for t in range(PACK)]
 
-        def fetch_h(t, lo, hi):
-            nc.scalar.activation(h_windows[t][:, lo:hi], h_banks[t][:, lo:hi], COPY, scale=-1.0)
-            nc.scalar.activation(h_own[t][:, lo:hi], h_banks[t][:, lo:hi], COPY)
+        z_codes = held.tile([P, S], I32, name="z_codes", align_bytes=64)
+        z_scales = held.tile([P, S], U8, name="z_scales", align_bytes=64)
+
+        h_banks = {}
+
+        def h_product(t, lo, hi, tag):
+            h_banks[t, lo] = psum.tile([P, hi - lo], F32, name="h_bank", tag=tag)
+            product(h_banks[t, lo][:], w2, t, z_codes[:, lo:hi], z_scales[:, lo:hi])
+            nc.scalar.activation(h_windows[t][:, lo:hi], h_banks[t, lo][:], COPY, scale=-1.0)
+
+        def h_keep(t, lo, hi):
+            nc.scalar.activation(h_own[t][:, lo:hi], h_banks[t, lo][:], COPY)
 
         def second_layer(lo, hi):
-            codes = held.tile([P, hi - lo], I32, name="z_codes%d" % lo, align_bytes=64)
-            scales = held.tile([P, hi - lo], U8, name="z_scales%d" % lo, align_bytes=64)
             grouped = z_grouped[starts.index(lo)]
-            nc.vector.quantize_mx(out=codes[:].bitcast(FP8X4), scales=scales[:], in_=grouped[:].rearrange("p c t -> p (c t)"))
-            for t in range(PACK):
-                product(h_banks[t][:, lo:hi], w2, t, codes[:], scales[:])
-            fetch_h(0, lo, hi)
+            nc.vector.quantize_mx(
+                out=z_codes[:, lo:hi].bitcast(FP8X4), scales=z_scales[:, lo:hi], in_=grouped[:].rearrange("p c t -> p (c t)")
+            )
+            h_product(0, lo, hi, "bank1_%d" % starts.index(lo))
+            if lo == 0:
+                h_keep(0, lo, hi)
 
         work = {}
 
         def scratch(kind, u):
-            tile = ring.tile([P, S], F32, name=kind)
+            if (kind, u) == ("top", len(units) - 1):
+                tile = held.tile([P, S], F32, name=kind, tag="z_grouped0", align_bytes=64)
+            else:
+                tile = ring.tile([P, S], F32, name=kind)
             work[kind, u] = tile[:, : units[u][2] - units[u][1]]
             return work[kind, u]
 
-        def looked_up(tiles, u, lst):
+        def look_up(kind, u, tables, lst, plain, op):
             t, lo, hi = units[u]
-            return tiles[t][:].indirect(entries(lst, lo, hi))
+            out = scratch(kind, u)
+            for a, b in halves if u == 0 else [(lo, hi)]:
+                nc.vector.tensor_tensor(out[:, a - lo : b - lo], tables[t][:].indirect(entries(lst, a, b)), plain[t][:, a:b], op)
 
         def at_place(tiles, u):
             t, lo, hi = units[u]
@@ -184,17 +203,20 @@ def tile_picked_layrangeunder_none_po_kernel(
 
         pipeline(
             [
-                (0, lambda u: nc.vector.tensor_tensor(scratch("da", u), looked_up(windows, u, list1), at_place(own, u), ALU.subtract)),
                 (1, lambda u: nc.vector.scalar_tensor_tensor(scratch("top", u), work["da", u], 0.0, work["db", u], ALU.max, ALU.max)),
-                (2, lambda u: nc.vector.scalar_tensor_tensor(scratch("spread", u), work["top", u], 2.0, work["low", u], ALU.mult, ALU.subtract)),
-                (0, lambda u: nc.vector.tensor_tensor(scratch("db", u), looked_up(windows, u, list2), at_place(own, u), ALU.subtract)),
-                (1, lambda u: nc.vector.scalar_tensor_tensor(scratch("low", u), work["da", u], 0.0, work["db", u], ALU.min, ALU.min)),
                 (2, finish_z),
+                (0, lambda u: look_up("da", u, windows, list1, own, ALU.subtract)),
+                (1, lambda u: nc.vector.scalar_tensor_tensor(scratch("low", u), work["da", u], 0.0, work["db", u], ALU.min, ALU.min)),
+                (0, lambda u: look_up("db", u, windows, list2, own, ALU.subtract)),
+                (1, lambda u: nc.vector.scalar_tensor_tensor(scratch("spread", u), work["top", u], 2.0, work["low", u], ALU.mult, ALU.subtract)),
             ]
         )
 
+        for lo, hi in chunks[1:]:
+            h_keep(0, lo, hi)
         for t in range(1, PACK):
-            fetch_h(t, 0, S)
+            h_product(t, 0, S, "bank0_%d" % t)
+            h_keep(t, 0, S)
 
         out_rows = out_0.rearrange("(p t) s -> p t s", t=PACK)
         out_words = out_1[0].rearrange("p c r -> p (c r)").bitcast(I32)
@@ -217,9 +239,9 @@ def tile_picked_layrangeunder_none_po_kernel(
 
         pipeline(
             [
-                (0, lambda u: nc.vector.tensor_tensor(scratch("ha", u), looked_up(h_windows, u, list3), at_place(h_own, u), ALU.add)),
+                (0, lambda u: look_up("ha", u, h_windows, list3, h_own, ALU.add)),
                 (1, finish_out),
-                (0, lambda u: nc.vector.tensor_tensor(scratch("hb", u), looked_up(h_windows, u, list4), at_place(h_own, u), ALU.add)),
+                (0, lambda u: look_up("hb", u, h_windows, list4, h_own, ALU.add)),
             ]
         )
         for q in range(QUADS):

@@ -1,6 +1,7 @@
 from contextlib import ExitStack
 
 import concourse.mybir as mybir
+from concourse.masks import make_identity
 
 K, T, S, H, N = 512, 2048, 512, 512, 512
 FLOPS = 2 * K * H * S + 2 * H * N * S
@@ -15,11 +16,13 @@ FP8X4 = mybir.dt.float8_e4m3fn_x4
 FP4X4 = mybir.dt.float4_e2m1fn_x4
 ALU = mybir.AluOpType
 COPY = mybir.ActivationFunctionType.Copy
+RELU = mybir.ActivationFunctionType.Relu
 
 P = 128
 PACK = 4
 QUADS = 4
 HALF = S // 2
+TURNED = 3
 PIECES = [256,128,128]
 
 
@@ -73,6 +76,9 @@ def tile_picked_layrangeunder_none_po_kernel(
             if width > S:
                 nc.gpsimd.memset(windows[t][:, S:], 0.0)
 
+        identity = held.tile([P, P], F32, name="identity")
+        make_identity(nc, identity[:])
+
         def deal(name, raw_words, raw_scales, scale_engine):
             words = held.tile([P, PACK, 2 * P], U8, name=name + "_words", align_bytes=64)
             scales = held.tile([P, PACK, P], U8, name=name + "_scales", align_bytes=64)
@@ -115,18 +121,20 @@ def tile_picked_layrangeunder_none_po_kernel(
         units = [(t, 0, S) for t in range(PACK - 1)] + [(PACK - 1, lo, hi) for lo, hi in chunks]
 
         own = [held.tile([P, S], F32, name="own%d" % t) for t in range(PACK)]
-        gained = [held.tile([P, S], F32, name="gained%d" % t) for t in range(PACK)]
-        for t in range(PACK):
-            for c in range(2):
-                lo, hi = c * HALF, (c + 1) * HALF
+        gained = {t: held.tile([P, S], F32, name="gained%d" % t) for t in range(TURNED, PACK)}
+
+        def fetch_y(t):
+            for c, (lo, hi) in enumerate(halves):
                 nc.scalar.activation(windows[t][:, lo:hi], y_banks[c, t][:], COPY, scale=0.5)
                 if (t, c) == (0, 0):
                     nc.vector.tensor_scalar(own[t][:, lo:hi], y_banks[c, t][:], 0.5, None, ALU.mult)
                 else:
                     nc.scalar.activation(own[t][:, lo:hi], y_banks[c, t][:], COPY, scale=0.5)
-            if t > 0:
-                nc.scalar.activation(gained[t - 1][:], own[t - 1][:], COPY, scale=gain[:, t - 1 : t])
-        nc.scalar.activation(gained[PACK - 1][:], own[PACK - 1][:], COPY, scale=gain[:, PACK - 1 : PACK])
+            if t >= TURNED:
+                nc.scalar.activation(gained[t][:], own[t][:], COPY, scale=gain[:, t : t + 1])
+
+        fetch_y(0)
+        fetch_y(1)
 
         def grouped_tiles(name):
             return [held.tile([P, hi - lo, PACK], BF16, name="%s%d" % (name, lo), align_bytes=64) for lo, hi in chunks]
@@ -191,11 +199,49 @@ def tile_picked_layrangeunder_none_po_kernel(
                     if 0 <= step - lag < len(units):
                         emit(step - lag)
 
+        def first_difference(u):
+            look_up("da", u, windows, list1, own, ALU.subtract)
+            if u < TURNED:
+                nc.scalar.activation(scratch("under", u), work["da", u], RELU, scale=-1.0)
+            if u == 0:
+                for t in range(2, PACK):
+                    fetch_y(t)
+
+        def sum_by_transposes(u):
+            t = u
+            for c, (lo, hi) in enumerate(halves):
+                total = psum.tile([P, HALF], F32, name="total", tag="bank%d_%d" % (c, t))
+                for j in range(0, HALF, P):
+                    terms = [own[t][:], work["top", u], work["top", u], work["low", u]]
+                    for i, term in enumerate(terms):
+                        nc.tensor.matmul(
+                            total[:, j : j + P], term[:, lo + j : lo + j + P], identity[:],
+                            start=i == 0, stop=i == len(terms) - 1, is_transpose=True,
+                        )
+                turned = ring.tile([P, HALF], F32, name="turned")
+                nc.scalar.copy(out=turned[:], in_=total[:])
+                back = psum.tile([P, HALF], F32, name="back", tag="bank%d_%d" % (c, PACK - 1))
+                for j in range(0, HALF, P):
+                    nc.tensor.transpose(back[:, j : j + P], turned[:, j : j + P], identity[:])
+                nc.scalar.activation(z_pairs[t // 2][:, t % 2, lo:hi], back[:], COPY, scale=gain[:, t : t + 1])
+
+        def low_side(u):
+            if u < TURNED:
+                nc.vector.scalar_tensor_tensor(scratch("low", u), work["db", u], -1.0, work["under", u], ALU.mult, ALU.max)
+                sum_by_transposes(u)
+            else:
+                nc.vector.scalar_tensor_tensor(scratch("low", u), work["da", u], 0.0, work["db", u], ALU.min, ALU.min)
+
+        def spread(u):
+            if u >= TURNED:
+                nc.vector.scalar_tensor_tensor(scratch("spread", u), work["top", u], 2.0, work["low", u], ALU.mult, ALU.subtract)
+
         def finish_z(u):
             t, lo, hi = units[u]
-            nc.vector.scalar_tensor_tensor(
-                z_pairs[t // 2][:, t % 2, lo:hi], work["spread", u], gain[:, t : t + 1], at_place(gained, u), ALU.mult, ALU.add
-            )
+            if u >= TURNED:
+                nc.vector.scalar_tensor_tensor(
+                    z_pairs[t // 2][:, t % 2, lo:hi], work["spread", u], gain[:, t : t + 1], at_place(gained, u), ALU.mult, ALU.add
+                )
             if t % 2:
                 round_pair(z_grouped, z_pairs[t // 2], units[u])
             if t == PACK - 1:
@@ -205,10 +251,10 @@ def tile_picked_layrangeunder_none_po_kernel(
             [
                 (1, lambda u: nc.vector.scalar_tensor_tensor(scratch("top", u), work["da", u], 0.0, work["db", u], ALU.max, ALU.max)),
                 (2, finish_z),
-                (0, lambda u: look_up("da", u, windows, list1, own, ALU.subtract)),
-                (1, lambda u: nc.vector.scalar_tensor_tensor(scratch("low", u), work["da", u], 0.0, work["db", u], ALU.min, ALU.min)),
+                (0, first_difference),
+                (1, low_side),
                 (0, lambda u: look_up("db", u, windows, list2, own, ALU.subtract)),
-                (1, lambda u: nc.vector.scalar_tensor_tensor(scratch("spread", u), work["top", u], 2.0, work["low", u], ALU.mult, ALU.subtract)),
+                (1, spread),
             ]
         )
 

from contextlib import ExitStack

import concourse.mybir as mybir
from concourse.masks import make_identity

K, T, S, H, N = 512, 2048, 512, 512, 512
FLOPS = 2 * K * H * S + 2 * H * N * S

F32 = mybir.dt.float32
BF16 = mybir.dt.bfloat16
I32 = mybir.dt.int32
U32 = mybir.dt.uint32
U16 = mybir.dt.uint16
U8 = mybir.dt.uint8
FP8X4 = mybir.dt.float8_e4m3fn_x4
FP4X4 = mybir.dt.float4_e2m1fn_x4
ALU = mybir.AluOpType
COPY = mybir.ActivationFunctionType.Copy
RELU = mybir.ActivationFunctionType.Relu

P = 128
PACK = 4
QUADS = 4
HALF = S // 2
TURNED = 3
PIECES = [256,128,128]


def tile_picked_layrangeunder_none_po_kernel(
    tc, x_words, x_scales, w1_words, w1_scales, gn, w2_words, w2_scales, offs, n1, n2, n3, n4, out_0, out_1, out_2
):
    nc = tc.nc
    with ExitStack() as ctx:
        held = ctx.enter_context(tc.tile_pool(name="held", bufs=1))
        ring = ctx.enter_context(tc.tile_pool(name="ring", bufs=3))
        psum = ctx.enter_context(tc.psum_pool(name="psum", bufs=1))

        def entries(lst, lo, hi):
            return lst[:, lo // 16 : hi // 16]

        def load_scale_rows(queues, tile, lo, scales):
            for q, queue in enumerate(queues):
                queue.dma_start(
                    out=tile[32 * q : 32 * q + 4, lo : lo + scales.shape[2]].bitcast(I32), in_=scales[0, 4 * q : 4 * q + 4, :].bitcast(I32)
                )

        def load_list(name, src):
            tile = held.tile([P, S // 16], U16, name="list_" + name)
            nc.sync.dma_start(tile[:], src)
            return tile

        x_scale_table = held.tile([P, T], U8, name="x_scale_table", align_bytes=64)
        x_word_table = held.tile([P, T], I32, name="x_word_table", align_bytes=64)
        w_scale_raw = held.tile([P, H + N], U8, name="w_scale_raw")
        w1_word_raw = held.tile([P, 2 * H], U8, name="w1_word_raw")
        w2_word_raw = held.tile([P, 2 * N], U8, name="w2_word_raw")
        gain = held.tile([P, PACK], F32, name="gain")
        nc.gpsimd.memset(x_scale_table[:].bitcast(I32), 0)
        nc.gpsimd.memset(w_scale_raw[:].bitcast(I32), 0)

        picked = load_list("offs", offs)
        nc.sync.dma_start(out=w1_word_raw[:].bitcast(I32), in_=w1_words[0].bitcast(I32))
        load_scale_rows([nc.sync, nc.sync, nc.scalar, nc.scalar], x_scale_table, 0, x_scales)
        nc.sync.dma_start(out=x_word_table[:], in_=x_words[0].rearrange("p c r -> p (c r)").bitcast(I32))
        load_scale_rows([nc.scalar] * QUADS, w_scale_raw, 0, w1_scales)
        list1, list2 = load_list("n1", n1), load_list("n2", n2)
        nc.sync.dma_start(out=w2_word_raw[:].bitcast(I32), in_=w2_words[0].bitcast(I32))
        nc.sync.dma_start(out=gain[:], in_=gn.rearrange("(p t) o -> p (t o)", t=PACK))
        load_scale_rows([nc.sync] * QUADS, w_scale_raw, H, w2_scales)
        list3, list4 = load_list("n3", n3), load_list("n4", n4)

        windows = []
        for t in range(PACK):
            width = S if t == PACK - 1 else 2 * S
            windows.append(held.tile([P, width], F32, name="window%d" % t))
            if width > S:
                nc.gpsimd.memset(windows[t][:, S:], 0.0)

        identity = held.tile([P, P], F32, name="identity")
        make_identity(nc, identity[:])

        def deal(name, raw_words, raw_scales, scale_engine):
            words = held.tile([P, PACK, 2 * P], U8, name=name + "_words", align_bytes=64)
            scales = held.tile([P, PACK, P], U8, name=name + "_scales", align_bytes=64)
            nc.vector.tensor_copy(
                out=words[:].rearrange("p t (m b) -> p t m b", b=2),
                in_=raw_words.rearrange("p (m t b) -> p t m b", t=PACK, b=2),
            )
            scale_engine.tensor_copy(out=scales[:], in_=raw_scales.rearrange("p (m t) -> p t m", t=PACK))
            return words, scales

        def product(bank, weights, t, codes, scales):
            nc.tensor.matmul_mx(
                out=bank,
                lhsT=weights[0][:, t, :].bitcast(FP4X4),
                lhsT_scale=weights[1][:, t, :],
                rhs=codes.bitcast(FP8X4),
                rhs_scale=scales,
                start=True,
                stop=True,
            )

        x_scale = held.tile([P, S], U8, name="x_scale", align_bytes=64)
        nc.vector.tensor_copy(out=x_scale[:], in_=x_scale_table[:].indirect(picked[:]))
        w1 = deal("w1", w1_word_raw[:], w_scale_raw[:, :H], nc.gpsimd)

        halves = [(0, HALF), (HALF, S)]
        x_codes = []
        for lo, hi in halves:
            x_codes.append(held.tile([P, HALF], I32, name="x_code%d" % lo, align_bytes=64))
            nc.vector.tensor_copy(out=x_codes[-1][:].bitcast(U32), in_=x_word_table[:].bitcast(U32).indirect(entries(picked, lo, hi)))
        y_banks = {}
        for t in range(PACK):
            for c, (lo, hi) in enumerate(halves):
                y_banks[c, t] = psum.tile([P, HALF], F32, name="y_bank", tag="bank%d_%d" % (c, t))
                product(y_banks[c, t][:], w1, t, x_codes[c][:], x_scale[:, lo:hi])
        w2 = deal("w2", w2_word_raw[:], w_scale_raw[:, H:], nc.vector)

        starts = [sum(PIECES[:i]) for i in range(len(PIECES))]
        chunks = [(lo, lo + width) for lo, width in zip(starts, PIECES)]
        units = [(t, 0, S) for t in range(PACK - 1)] + [(PACK - 1, lo, hi) for lo, hi in chunks]

        own = [held.tile([P, S], F32, name="own%d" % t) for t in range(PACK)]
        gained = {t: held.tile([P, S], F32, name="gained%d" % t) for t in range(TURNED, PACK)}

        def fetch_y(t):
            for c, (lo, hi) in enumerate(halves):
                nc.scalar.activation(windows[t][:, lo:hi], y_banks[c, t][:], COPY, scale=0.5)
                if (t, c) == (0, 0):
                    nc.vector.tensor_scalar(own[t][:, lo:hi], y_banks[c, t][:], 0.5, None, ALU.mult)
                else:
                    nc.scalar.activation(own[t][:, lo:hi], y_banks[c, t][:], COPY, scale=0.5)
            if t >= TURNED:
                nc.scalar.activation(gained[t][:], own[t][:], COPY, scale=gain[:, t : t + 1])

        fetch_y(0)
        fetch_y(1)

        def grouped_tiles(name):
            return [held.tile([P, hi - lo, PACK], BF16, name="%s%d" % (name, lo), align_bytes=64) for lo, hi in chunks]

        def round_pair(grouped, pair, unit):
            t, lo, hi = unit
            for tile, (c_lo, c_hi) in zip(grouped, chunks):
                if lo <= c_lo and c_hi <= hi:
                    copy = nc.vector.tensor_copy if (t, hi) == (PACK - 1, S) else nc.scalar.copy
                    copy(out=tile[:, :, t - 1 : t + 1], in_=pair[:, :, c_lo:c_hi].rearrange("p t s -> p s t"))

        h_windows = windows[:-1] + [held.tile([P, S], F32, name="h_window_last")]
        h_own = own[:-1] + [held.tile([P, S], F32, name="h_own_last")]
        z_pairs = [held.tile([P, 2, S], F32, name="z_pair%d" % i) for i in range(2)]
        z_grouped = grouped_tiles("z_grouped")

        z_codes = held.tile([P, S], I32, name="z_codes", align_bytes=64)
        z_scales = held.tile([P, S], U8, name="z_scales", align_bytes=64)

        h_banks = {}

        def h_product(t, lo, hi, tag):
            h_banks[t, lo] = psum.tile([P, hi - lo], F32, name="h_bank", tag=tag)
            product(h_banks[t, lo][:], w2, t, z_codes[:, lo:hi], z_scales[:, lo:hi])
            nc.scalar.activation(h_windows[t][:, lo:hi], h_banks[t, lo][:], COPY, scale=-1.0)

        def h_keep(t, lo, hi):
            nc.scalar.activation(h_own[t][:, lo:hi], h_banks[t, lo][:], COPY)

        def second_layer(lo, hi):
            grouped = z_grouped[starts.index(lo)]
            nc.vector.quantize_mx(
                out=z_codes[:, lo:hi].bitcast(FP8X4), scales=z_scales[:, lo:hi], in_=grouped[:].rearrange("p c t -> p (c t)")
            )
            h_product(0, lo, hi, "bank1_%d" % starts.index(lo))
            if lo == 0:
                h_keep(0, lo, hi)

        work = {}

        def scratch(kind, u):
            if (kind, u) == ("top", len(units) - 1):
                tile = held.tile([P, S], F32, name=kind, tag="z_grouped0", align_bytes=64)
            else:
                tile = ring.tile([P, S], F32, name=kind)
            work[kind, u] = tile[:, : units[u][2] - units[u][1]]
            return work[kind, u]

        def look_up(kind, u, tables, lst, plain, op):
            t, lo, hi = units[u]
            out = scratch(kind, u)
            for a, b in halves if u == 0 else [(lo, hi)]:
                nc.vector.tensor_tensor(out[:, a - lo : b - lo], tables[t][:].indirect(entries(lst, a, b)), plain[t][:, a:b], op)

        def at_place(tiles, u):
            t, lo, hi = units[u]
            return tiles[t][:, lo:hi]

        def pipeline(slots):
            for step in range(len(units) + max(lag for lag, emit in slots)):
                for lag, emit in slots:
                    if 0 <= step - lag < len(units):
                        emit(step - lag)

        def first_difference(u):
            look_up("da", u, windows, list1, own, ALU.subtract)
            if u < TURNED:
                nc.scalar.activation(scratch("under", u), work["da", u], RELU, scale=-1.0)
            if u == 0:
                for t in range(2, PACK):
                    fetch_y(t)

        def sum_by_transposes(u):
            t = u
            for c, (lo, hi) in enumerate(halves):
                total = psum.tile([P, HALF], F32, name="total", tag="bank%d_%d" % (c, t))
                for j in range(0, HALF, P):
                    terms = [own[t][:], work["top", u], work["top", u], work["low", u]]
                    for i, term in enumerate(terms):
                        nc.tensor.matmul(
                            total[:, j : j + P], term[:, lo + j : lo + j + P], identity[:],
                            start=i == 0, stop=i == len(terms) - 1, is_transpose=True,
                        )
                turned = ring.tile([P, HALF], F32, name="turned")
                nc.scalar.copy(out=turned[:], in_=total[:])
                back = psum.tile([P, HALF], F32, name="back", tag="bank%d_%d" % (c, PACK - 1))
                for j in range(0, HALF, P):
                    nc.tensor.transpose(back[:, j : j + P], turned[:, j : j + P], identity[:])
                nc.scalar.activation(z_pairs[t // 2][:, t % 2, lo:hi], back[:], COPY, scale=gain[:, t : t + 1])

        def low_side(u):
            if u < TURNED:
                nc.vector.scalar_tensor_tensor(scratch("low", u), work["db", u], -1.0, work["under", u], ALU.mult, ALU.max)
                sum_by_transposes(u)
            else:
                nc.vector.scalar_tensor_tensor(scratch("low", u), work["da", u], 0.0, work["db", u], ALU.min, ALU.min)

        def spread(u):
            if u >= TURNED:
                nc.vector.scalar_tensor_tensor(scratch("spread", u), work["top", u], 2.0, work["low", u], ALU.mult, ALU.subtract)

        def finish_z(u):
            t, lo, hi = units[u]
            if u >= TURNED:
                nc.vector.scalar_tensor_tensor(
                    z_pairs[t // 2][:, t % 2, lo:hi], work["spread", u], gain[:, t : t + 1], at_place(gained, u), ALU.mult, ALU.add
                )
            if t % 2:
                round_pair(z_grouped, z_pairs[t // 2], units[u])
            if t == PACK - 1:
                second_layer(lo, hi)

        pipeline(
            [
                (1, lambda u: nc.vector.scalar_tensor_tensor(scratch("top", u), work["da", u], 0.0, work["db", u], ALU.max, ALU.max)),
                (2, finish_z),
                (0, first_difference),
                (1, low_side),
                (0, lambda u: look_up("db", u, windows, list2, own, ALU.subtract)),
                (1, spread),
            ]
        )

        for lo, hi in chunks[1:]:
            h_keep(0, lo, hi)
        for t in range(1, PACK):
            h_product(t, 0, S, "bank0_%d" % t)
            h_keep(t, 0, S)

        out_rows = out_0.rearrange("(p t) s -> p t s", t=PACK)
        out_words = out_1[0].rearrange("p c r -> p (c r)").bitcast(I32)
        out_scales = held.tile([P, S], U8, name="out_scales", align_bytes=64)
        out_pairs = [held.tile([P, 2, S], F32, name="out_pair%d" % i) for i in range(2)]
        out_grouped = grouped_tiles("out_grouped")

        def finish_out(u):
            t, lo, hi = units[u]
            result = out_pairs[t // 2][:, t % 2, lo:hi]
            nc.vector.tensor_tensor(result, work["ha", u], work["hb", u], ALU.max)
            if t % 2:
                round_pair(out_grouped, out_pairs[t // 2], units[u])
            nc.sync.dma_start(out=out_rows[:, t, lo:hi], in_=result)
            if t == PACK - 1:
                codes = held.tile([P, hi - lo], I32, name="out_codes%d" % lo, align_bytes=64)
                grouped = out_grouped[starts.index(lo)]
                nc.vector.quantize_mx(out=codes[:].bitcast(FP8X4), scales=out_scales[:, lo:hi], in_=grouped[:].rearrange("p c t -> p (c t)"))
                nc.sync.dma_start(out=out_words[:, lo:hi], in_=codes[:])

        pipeline(
            [
                (0, lambda u: look_up("ha", u, h_windows, list3, h_own, ALU.add)),
                (1, finish_out),
                (0, lambda u: look_up("hb", u, h_windows, list4, h_own, ALU.add)),
            ]
        )
        for q in range(QUADS):
            engine = nc.scalar if q % 2 else nc.sync
            engine.dma_start(out=out_2[0, 4 * q : 4 * q + 4, :].bitcast(I32), in_=out_scales[32 * q : 32 * q + 4, :].bitcast(I32))
